import numpy as np
import ml_dtypes


def mxq(x, axis, fmt="e4m3"):
    dtype, down = {"e4m3": (ml_dtypes.float8_e4m3fn, 7), "e5m2": (ml_dtypes.float8_e5m2, 14)}[fmt]
    v = np.moveaxis(np.asarray(x, np.float32).astype(ml_dtypes.bfloat16).astype(np.float64), axis, -1)
    blocks = v.reshape(v.shape[:-1] + (-1, 32))
    amax = np.abs(blocks).max(-1, keepdims=True)
    byte = np.maximum(np.where(amax > 0, np.frexp(amax)[1] - 1 + 127, 0) - down, 1)
    scale = np.exp2(byte - 127.0)
    codes = (blocks / scale).astype(np.float32).astype(dtype).astype(np.float64)
    return np.moveaxis((codes * scale).reshape(v.shape), -1, axis)


WIDE = False


def mx_kscale(k):
    if not WIDE:
        return np.ones(k)
    levels = np.array([10, -10, 5, -5, 0])
    if k % 512:
        return np.exp2(np.random.permutation(np.resize(levels, k // 32))).repeat(32)
    a = np.empty((k // 512, 16))
    for p in range(k // 512):
        a[p, :8] = np.random.permutation(np.resize(levels, 8))
        for g in range(8):
            far = levels[np.abs(levels - a[p, g]) >= 10]
            a[p, g + 8] = far[np.random.randint(len(far))]
    return np.exp2(a.ravel()).repeat(32)


def f64(x):
    return np.asarray(x).astype(np.float64)


def striped(idx):
    return np.tile(np.asarray(idx).reshape(-1, 16).T, (8, 1)).astype(np.uint16)


def unstriped(offs):
    return offs[:16].T.reshape(-1).astype(np.int64)


E2M1 = np.array([0.0, 0.5, 1.0, 1.5, 2.0, 3.0, 4.0, 6.0, -0.0, -0.5, -1.0, -1.5, -2.0, -3.0, -4.0, -6.0])


def pack_weight(w, fmt):
    k, n = w.shape
    w = f64(np.asarray(w, np.float32).astype(ml_dtypes.bfloat16)).reshape(k // 32, 32, n)
    amax = np.abs(w).max(1)
    if fmt == "e4m3":
        byte = np.frexp(amax)[1] - 1 + 127 - 7
    else:
        mant, ex = np.frexp(amax / 6.0)
        byte = np.where(mant > 0.5, ex, ex - 1) + 127
    byte = np.clip(np.where(amax > 0, byte, 1), 1, 254)
    scaled = (w * np.exp2(127.0 - byte)[:, None, :]).reshape(k, n).astype(np.float32)
    by_word = np.ascontiguousarray(scaled.reshape(k // 512, 128, 4, n).transpose(0, 1, 3, 2))
    if fmt == "e4m3":
        words = by_word.astype(ml_dtypes.float8_e4m3fn).view(np.uint8)
    else:
        c = by_word.astype(ml_dtypes.float4_e2m1fn).view(np.uint8) & 0xF
        words = (c[..., 0::2] | (c[..., 1::2] << 4)).reshape(k // 512, 128, 2 * n)
    return np.ascontiguousarray(words), np.ascontiguousarray(byte.astype(np.uint8).reshape(k // 512, 16, n))


def unpack_weight(words, scales, fmt):
    g, _, n = scales.shape
    words = np.ascontiguousarray(words).reshape(g, 128, n, -1)
    if fmt == "e4m3":
        vals = words.view(ml_dtypes.float8_e4m3fn).astype(np.float64)
    else:
        nib = np.empty((g, 128, n, 4), np.uint8)
        nib[..., 0::2] = words & 0xF
        nib[..., 1::2] = words >> 4
        vals = E2M1[nib]
    vals = vals * np.repeat(np.exp2(scales.astype(np.float64) - 127.0), 8, axis=1)[..., None]
    return vals.transpose(0, 1, 3, 2).reshape(g * 512, n)


def silu(v):
    return v / (1.0 + np.exp(-v))


D, K, R, T, I, Q, G = 512, 512, 512, 2048, 512, 128, 32


def setup_inputs():
    n = np.random.standard_normal
    idx = np.random.permutation(T)[:I]
    fd = mx_kscale(D)
    fk = mx_kscale(K)
    fr = mx_kscale(R)
    keysp = pack_weight(n((D, T)) / fd[:, None], "e2m1")
    tabp = pack_weight(n((K, T)) / fk[:, None], "e2m1")
    return {
        "query": (n((D, Q)) * 0.7 / np.sqrt(D) * fd[:, None]).astype(np.float32),
        "keys_words": keysp[0],
        "keys_scales": keysp[1],
        "tab_words": tabp[0],
        "tab_scales": tabp[1],
        "w1": (n((K, R)) * 1 / np.sqrt(K) * fk[:, None]).astype(np.float32),
        "gain": (np.random.uniform(0.7, 2.0, (R, 1))).astype(np.float32),
        "gout": (n((R, Q)) * 1 / np.sqrt(R) * fr[:, None]).astype(np.float32),
        "hsc": (np.random.uniform(0.7, 1.4, (R, 1)) / fr[:, None]).astype(np.float32),
        "old": (0.5 * n((Q, T))).astype(np.float32),
        "offs": striped(idx),
    }


def reference(query, keys_words, keys_scales, tab_words, tab_scales, w1, gain, gout, hsc, old, offs):
    idx = unstriped(offs)
    keysu = unpack_weight(keys_words, keys_scales, "e2m1")
    tabu = unpack_weight(tab_words, tab_scales, "e2m1")
    queryq = mxq(f64(query), 0, "e4m3")
    keysidxg = keysu[:, idx]
    a = queryq.T @ keysidxg
    p = np.exp(a - np.max(a, axis=1, keepdims=True))
    z = np.sum(p, axis=1, keepdims=True)
    w1q = mxq(f64(w1), 0, "e4m3")
    tabidxg = tabu[:, idx]
    zh = w1q.T @ tabidxg
    mz = np.sqrt(np.square(zh).reshape(R, G, I // G).mean(axis=2) + 0.1)
    mzr = np.repeat(mz, I // G, axis=1)
    hv = silu(zh / mzr * f64(gain))
    hs1 = hv * f64(hsc)
    goutq = mxq(f64(gout), 0, "e4m3")
    hs1q = mxq(hs1, 0, "e4m3")
    c0 = goutq.T @ hs1q
    dz = np.sum(c0 * p / np.square(z) * (-1.0), axis=1, keepdims=True)
    dp = c0 / z + dz
    da = dp * p
    gs = da * 512.0
    gf = np.zeros((Q, T))
    gf[:, idx] = gs
    y = f64(old) + gf
    return y

@@ -1,0 +1,246 @@
+from contextlib import ExitStack
+
+import concourse.mybir as mybir
+from concourse.masks import make_identity
+
+F32 = mybir.dt.float32
+BF16 = mybir.dt.bfloat16
+I32 = mybir.dt.int32
+U32 = mybir.dt.uint32
+U16 = mybir.dt.uint16
+U8 = mybir.dt.uint8
+FP8X4 = mybir.dt.float8_e4m3fn_x4
+FP4X4 = mybir.dt.float4_e2m1fn_x4
+ALU = mybir.AluOpType
+ACT = mybir.ActivationFunctionType
+AXIS = mybir.AxisListType
+
+P = 128
+PACK = 4
+T = 2048
+SLOTS = 512
+R = 512
+Q = 128
+PAGE = 16
+CHUNK = 128
+CHUNKS = SLOTS // CHUNK
+PAGES = CHUNK // PAGE
+OUT_COLS = (256, 512, 512, 512, 256)
+
+FLOPS = 2 * 512 * SLOTS * (Q + R + Q)
+
+
+def tile_attend_blrscaled_soft_kernel(tc, query, keys_words, keys_scales, tab_words, tab_scales, w1, gain, gout, hsc, old, offs, out):
+    nc = tc.nc
+    with ExitStack() as ctx:
+        sb = ctx.enter_context(tc.tile_pool(name="sb", bufs=1))
+        ps = ctx.enter_context(tc.psum_pool(name="ps", bufs=1))
+
+        def tile(name, shape, dtype, tag=None):
+            return sb.tile(shape, dtype, name=name, tag=tag or name, align_bytes=64)
+
+        offsets = sb.tile([P, SLOTS // 16], U16, name="offsets")
+        tab_w = tile("tab_w", [P, T], U16)
+        tab_s = tile("tab_s", [P, T], U8)
+        key_w = tile("key_w", [P, T], U16)
+        key_s = tile("key_s", [P, T], U8)
+        window = tile("window", [P, T], F32)
+
+        nc.vector.memset(tab_s[:].bitcast(I32), 0)
+        nc.vector.memset(key_s[:].bitcast(I32), 0)
+        nc.vector.memset(window[:], 0.0)
+
+        def load_scales(dst, src):
+            rows = src[0].bitcast(I32)
+            for quad in range(4):
+                nc.sync.dma_start(out=dst[:].bitcast(I32)[32 * quad : 32 * quad + 4, :], in_=rows[4 * quad : 4 * quad + 4, :])
+
+        nc.sync.dma_start(offsets[:], offs)
+        nc.sync.dma_start(out=tab_w[:].bitcast(I32), in_=tab_words[0].bitcast(I32))
+        load_scales(tab_s, tab_scales)
+        half = R // 2
+        w_raw = [tile("w_raw%d" % h, [P, PACK, half], F32) for h in range(2)]
+        w_rows = w1.rearrange("(p j) r -> p j r", j=PACK)
+        for h in range(2):
+            nc.sync.dma_start(out=w_raw[h][:], in_=w_rows[:, :, h * half : (h + 1) * half])
+        q_raw = tile("q_raw", [P, PACK, Q], F32)
+        g_raw = tile("g_raw", [P, PACK, Q], F32)
+        nc.sync.dma_start(out=q_raw[:], in_=query.rearrange("(p j) q -> p j q", j=PACK))
+        nc.sync.dma_start(out=g_raw[:], in_=gout.rearrange("(p j) q -> p j q", j=PACK))
+        nc.sync.dma_start(out=key_w[:].bitcast(I32), in_=keys_words[0].bitcast(I32))
+        load_scales(key_s, keys_scales)
+        gain_sb = tile("gain_sb", [P, PACK], F32)
+        hsc_sb = tile("hsc_sb", [P, PACK], F32)
+        nc.sync.dma_start(out=gain_sb[:], in_=gain.rearrange("(p j) o -> p (j o)", j=PACK))
+        nc.sync.dma_start(out=hsc_sb[:], in_=hsc.rearrange("(p j) o -> p (j o)", j=PACK))
+        old_sb = tile("old_sb", [P, T], F32)
+        nc.sync.dma_start(out=old_sb[:], in_=old)
+
+        consts = tile("consts", [P, 2], F32)
+        nc.gpsimd.memset(consts[:, 0:1], 512.0)
+        nc.gpsimd.memset(consts[:, 1:2], -1.0)
+        ident = tile("ident", [P, P], F32)
+        make_identity(nc, ident[:])
+
+        def gather(name, src, dtype):
+            dst = tile(name, [P, SLOTS], dtype)
+            nc.vector.tensor_copy(dst[:], src[:].indirect(offsets[:]))
+            return dst
+
+        def quantise(name, src, words):
+            codes = tile(name + "_codes", [P, words], U32)
+            scales = tile(name + "_scales", [P, words], U8)
+            nc.vector.quantize_mx(out=codes[:].bitcast(FP8X4), scales=scales[:], in_=src)
+            return codes, scales
+
+        tab_wg = gather("tab_wg", tab_w, U16)
+        tab_sg = gather("tab_sg", tab_s, U8)
+
+        w_bf = tile("w_bf", [P, PACK, P, PACK], BF16)
+        mh = P // 2
+        nc.scalar.copy(
+            out=w_bf[:, :, 0:mh, :].rearrange("p t m j -> p m j t"),
+            in_=w_raw[0][:].rearrange("p j (m t) -> p m j t", t=PACK),
+        )
+        nc.vector.tensor_copy(
+            out=w_bf[:, :, mh:P, :].rearrange("p t m j -> p m j t"),
+            in_=w_raw[1][:].rearrange("p j (m t) -> p m j t", t=PACK),
+        )
+        w_mx = [quantise("w%d" % t, w_bf[:, t].rearrange("p m j -> p (m j)"), P) for t in range(PACK)]
+
+        q_bf = tile("q_bf", [P, Q, PACK], BF16)
+        g_bf = tile("g_bf", [P, Q, PACK], BF16)
+        for dst, src in ((q_bf, q_raw), (g_bf, g_raw)):
+            nc.scalar.copy(
+                out=dst[:].rearrange("p (c i) j -> p c j i", i=4),
+                in_=src[:].rearrange("p j (c i) -> p c j i", i=4),
+            )
+
+        zh = [ps.tile([P, PACK, CHUNK], F32, name="zh%d" % c) for c in range(CHUNKS)]
+        for c in range(CHUNKS):
+            cols = slice(c * CHUNK, (c + 1) * CHUNK)
+            for t in range(PACK):
+                nc.tensor.matmul_mx(
+                    out=zh[c][:, t, :],
+                    lhsT=w_mx[t][0][:].bitcast(FP8X4),
+                    lhsT_scale=w_mx[t][1][:],
+                    rhs=tab_wg[:, cols].bitcast(FP4X4),
+                    rhs_scale=tab_sg[:, cols],
+                    start=True,
+                    stop=True,
+                )
+
+        key_wg = gather("key_wg", key_w, U16)
+
+        key_sg = gather("key_sg", key_s, U8)
+        halves = 2
+        hj = PAGE // halves
+        sq = [tile("sq%d" % h, [P, hj, CHUNKS, PAGES, PACK], F32) for h in range(halves)]
+        mean_sq_t = ps.tile([P, P], F32, name="mean_sq_t")
+        for h in range(halves):
+            for c in range(CHUNKS):
+                nc.scalar.activation(
+                    out=sq[h][:, :, c],
+                    in_=zh[c][:].rearrange("p t (g j) -> p j g t", j=PAGE)[:, h * hj : (h + 1) * hj],
+                    func=ACT.Square,
+                    scale=0.25,
+                )
+            for j in range(hj):
+                nc.tensor.matmul(
+                    out=mean_sq_t[:],
+                    lhsT=sq[h][:, j].rearrange("p c g t -> p (c g t)"),
+                    rhs=ident[:],
+                    is_transpose=True,
+                    start=(h == 0 and j == 0),
+                    stop=(h == halves - 1 and j == hj - 1),
+                )
+        inv_rms_t = tile("inv_rms_t", [P, P], F32)
+        nc.scalar.activation(out=inv_rms_t[:], in_=mean_sq_t[:], func=ACT.Abs_reciprocal_sqrt, bias=0.1)
+        inv_rms = ps.tile([P, P], F32, name="inv_rms")
+        nc.tensor.transpose(inv_rms[:], inv_rms_t[:], ident[:])
+        q_codes, q_scales = quantise("q", q_bf[:].rearrange("p q j -> p (q j)"), Q)
+        g_codes, g_scales = quantise("g", g_bf[:].rearrange("p q j -> p (q j)"), Q)
+        scores = ps.tile([P, SLOTS], F32, name="scores")
+        nc.tensor.matmul_mx(
+            out=scores[:],
+            lhsT=q_codes[:].bitcast(FP8X4),
+            lhsT_scale=q_scales[:],
+            rhs=key_wg[:].bitcast(FP4X4),
+            rhs_scale=key_sg[:],
+            start=True,
+            stop=True,
+        )
+
+        neg_max = tile("neg_max", [P, 1], F32)
+        nc.vector.tensor_reduce(out=neg_max[:], in_=scores[:], axis=AXIS.X, op=ALU.max, negate=True)
+        factor = tile("factor", [P, CHUNKS * PAGES, PACK], F32)
+        nc.vector.tensor_tensor(
+            out=factor[:],
+            in0=inv_rms[:].rearrange("p (g t) -> p g t", t=PACK),
+            in1=gain_sb[:].rearrange("p (o t) -> p o t", o=1).to_broadcast([P, CHUNKS * PAGES, PACK]),
+            op=ALU.mult,
+        )
+
+        hv = []
+        for c in range(CHUNKS):
+            x = tile("x%d" % c, [P, PAGES, PAGE, PACK], F32)
+            nc.vector.tensor_tensor(
+                out=x[:],
+                in0=zh[c][:].rearrange("p t (g j) -> p g j t", j=PAGE),
+                in1=factor[:, c * PAGES : (c + 1) * PAGES, :].rearrange("p g (o t) -> p g o t", o=1).to_broadcast([P, PAGES, PAGE, PACK]),
+                op=ALU.mult,
+            )
+            hv.append(tile("hv%d" % c, [P, CHUNK, PACK], F32))
+            nc.scalar.activation(out=hv[c][:].rearrange("p n t -> p (n t)"), in_=x[:].rearrange("p g j t -> p (g j t)"), func=ACT.Silu)
+
+        h_bf = [tile("h_bf%d" % c, [P, CHUNK, PACK], BF16) for c in range(CHUNKS)]
+        c0 = ps.tile([P, SLOTS], F32, name="c0")
+
+        def scale_rows(c):
+            nc.vector.tensor_tensor(
+                out=h_bf[c][:],
+                in0=hv[c][:],
+                in1=hsc_sb[:].rearrange("p (o t) -> p o t", o=1).to_broadcast([P, CHUNK, PACK]),
+                op=ALU.mult,
+            )
+
+        def read_back(c):
+            h_codes, h_scales = quantise("h%d" % c, h_bf[c][:].rearrange("p n t -> p (n t)"), CHUNK)
+            nc.tensor.matmul_mx(
+                out=c0[:, c * CHUNK : (c + 1) * CHUNK],
+                lhsT=g_codes[:].bitcast(FP8X4),
+                lhsT_scale=g_scales[:],
+                rhs=h_codes[:].bitcast(FP8X4),
+                rhs_scale=h_scales[:],
+                start=True,
+                stop=True,
+            )
+
+        scale_rows(0)
+        for c in range(1, CHUNKS):
+            scale_rows(c)
+            read_back(c - 1)
+        read_back(CHUNKS - 1)
+
+        p = tile("p", [P, SLOTS], F32, tag="x%d" % (CHUNKS - 1))
+        z = tile("z", [P, 1], F32)
+        nc.scalar.activation(out=p[:], in_=scores[:], func=ACT.Exp, bias=neg_max[:], accum_out=z[:])
+        inv_z = tile("inv_z", [P, 1], F32)
+        nc.vector.reciprocal(out=inv_z[:], in_=z[:])
+        coef = tile("coef", [P, 2], F32)
+        nc.vector.tensor_scalar(out=coef[:], in0=consts[:], scalar1=inv_z[:], scalar2=None, op0=ALU.mult)
+
+        cp = tile("cp", [P, SLOTS], F32)
+        total = tile("total", [P, 1], F32)
+        nc.vector.scalar_tensor_tensor(out=cp[:], in0=c0[:], scalar=coef[:, 0:1], in1=p[:], op0=ALU.mult, op1=ALU.mult, accum_out=total[:])
+        shift = tile("shift", [P, SLOTS], F32)
+        nc.vector.tensor_scalar(out=shift[:], in0=p[:], scalar1=total[:], scalar2=coef[:, 1:2], op0=ALU.mult, op1=ALU.mult)
+        nc.vector.tensor_tensor(out=window[:].indirect(offsets[:]), in0=cp[:], in1=shift[:], op=ALU.add)
+
+        for n, width in enumerate(OUT_COLS):
+            first = sum(OUT_COLS[:n])
+            cols = slice(first, first + width)
+            res = tile("res%d" % n, [P, width], F32)
+            nc.vector.tensor_tensor(out=res[:], in0=window[:, cols], in1=old_sb[:, cols], op=ALU.add)
+            queue = nc.sync if n % 2 == 0 else nc.scalar
+            queue.dma_start(out=out[:, cols], in_=res[:])

@@ -79,6 +79,8 @@ def tile_attend_blrscaled_soft_kernel(tc, query, keys_words, keys_scales, tab_wo
         consts = tile("consts", [P, 2], F32)
         nc.gpsimd.memset(consts[:, 0:1], 512.0)
         nc.gpsimd.memset(consts[:, 1:2], -1.0)
+        warm = tile("warm", [P, 1], F32)
+        nc.scalar.activation(out=warm[:], in_=consts[:, 0:1], func=ACT.Abs_reciprocal_sqrt)
         ident = tile("ident", [P, P], F32)
         make_identity(nc, ident[:])
 
@@ -87,8 +89,8 @@ def tile_attend_blrscaled_soft_kernel(tc, query, keys_words, keys_scales, tab_wo
             nc.vector.tensor_copy(dst[:], src[:].indirect(offsets[:]))
             return dst
 
-        def quantise(name, src, words):
-            codes = tile(name + "_codes", [P, words], U32)
+        def quantise(name, src, words, tag=None):
+            codes = tile(name + "_codes", [P, words], U32, tag=tag)
             scales = tile(name + "_scales", [P, words], U8)
             nc.vector.quantize_mx(out=codes[:].bitcast(FP8X4), scales=scales[:], in_=src)
             return codes, scales
@@ -102,10 +104,10 @@ def tile_attend_blrscaled_soft_kernel(tc, query, keys_words, keys_scales, tab_wo
             out=w_bf[:, :, 0:mh, :].rearrange("p t m j -> p m j t"),
             in_=w_raw[0][:].rearrange("p j (m t) -> p m j t", t=PACK),
         )
-        nc.vector.tensor_copy(
-            out=w_bf[:, :, mh:P, :].rearrange("p t m j -> p m j t"),
-            in_=w_raw[1][:].rearrange("p j (m t) -> p m j t", t=PACK),
-        )
+        share = 20
+        late = w_raw[1][:].rearrange("p j (m t) -> p m j t", t=PACK)
+        nc.scalar.copy(out=w_bf[:, :, mh : mh + share, :].rearrange("p t m j -> p m j t"), in_=late[:, 0:share])
+        nc.vector.tensor_copy(out=w_bf[:, :, mh + share : P, :].rearrange("p t m j -> p m j t"), in_=late[:, share:mh])
         w_mx = [quantise("w%d" % t, w_bf[:, t].rearrange("p m j -> p (m j)"), P) for t in range(PACK)]
 
         q_bf = tile("q_bf", [P, Q, PACK], BF16)
@@ -117,7 +119,7 @@ def tile_attend_blrscaled_soft_kernel(tc, query, keys_words, keys_scales, tab_wo
             )
 
         zh = [ps.tile([P, PACK, CHUNK], F32, name="zh%d" % c) for c in range(CHUNKS)]
-        for c in range(CHUNKS):
+        for c in (1, 2, 3, 0):
             cols = slice(c * CHUNK, (c + 1) * CHUNK)
             for t in range(PACK):
                 nc.tensor.matmul_mx(
@@ -133,33 +135,39 @@ def tile_attend_blrscaled_soft_kernel(tc, query, keys_words, keys_scales, tab_wo
         key_wg = gather("key_wg", key_w, U16)
 
         key_sg = gather("key_sg", key_s, U8)
-        halves = 2
-        hj = PAGE // halves
-        sq = [tile("sq%d" % h, [P, hj, CHUNKS, PAGES, PACK], F32) for h in range(halves)]
+        early = (CHUNKS - 1) * PAGES * PACK
+        sq = tile("sq", [P, PAGE * early + P - early], F32)
+        nc.gpsimd.memset(sq[:, PAGE * early :], 0.0)
+        sq_view = sq[:, 0 : PAGE * early].rearrange("p (j c g t) -> p j c g t", j=PAGE, g=PAGES, t=PACK)
+        for c in range(1, CHUNKS):
+            nc.scalar.activation(
+                out=sq_view[:, :, c - 1],
+                in_=zh[c][:].rearrange("p t (g j) -> p j g t", j=PAGE),
+                func=ACT.Square,
+                scale=0.25,
+            )
+        sq_last = tile("sq_last", [P, PAGES, PACK, PAGE], F32)
+        nc.scalar.activation(out=sq_last[:], in_=zh[0][:].rearrange("p t (g j) -> p g t j", j=PAGE), func=ACT.Square, scale=0.25)
         mean_sq_t = ps.tile([P, P], F32, name="mean_sq_t")
-        for h in range(halves):
-            for c in range(CHUNKS):
-                nc.scalar.activation(
-                    out=sq[h][:, :, c],
-                    in_=zh[c][:].rearrange("p t (g j) -> p j g t", j=PAGE)[:, h * hj : (h + 1) * hj],
-                    func=ACT.Square,
-                    scale=0.25,
-                )
-            for j in range(hj):
-                nc.tensor.matmul(
-                    out=mean_sq_t[:],
-                    lhsT=sq[h][:, j].rearrange("p c g t -> p (c g t)"),
-                    rhs=ident[:],
-                    is_transpose=True,
-                    start=(h == 0 and j == 0),
-                    stop=(h == halves - 1 and j == hj - 1),
-                )
+        for j in range(PAGE):
+            nc.tensor.matmul(
+                out=mean_sq_t[:],
+                lhsT=sq[:, j * early : j * early + P],
+                rhs=ident[:],
+                is_transpose=True,
+                start=(j == 0),
+                stop=(j == PAGE - 1),
+            )
+        g_codes, g_scales = quantise("g", g_bf[:].rearrange("p q j -> p (q j)"), Q)
+        mean_sq = tile("mean_sq", [P, PAGES * PACK], F32)
+        nc.vector.tensor_reduce(out=mean_sq[:], in_=sq_last[:].rearrange("p g t j -> p (g t) j"), axis=AXIS.X, op=ALU.add)
         inv_rms_t = tile("inv_rms_t", [P, P], F32)
         nc.scalar.activation(out=inv_rms_t[:], in_=mean_sq_t[:], func=ACT.Abs_reciprocal_sqrt, bias=0.1)
+        inv_last = tile("inv_last", [P, PAGES * PACK], F32)
+        nc.scalar.activation(out=inv_last[:], in_=mean_sq[:], func=ACT.Abs_reciprocal_sqrt, bias=0.1)
         inv_rms = ps.tile([P, P], F32, name="inv_rms")
         nc.tensor.transpose(inv_rms[:], inv_rms_t[:], ident[:])
-        q_codes, q_scales = quantise("q", q_bf[:].rearrange("p q j -> p (q j)"), Q)
-        g_codes, g_scales = quantise("g", g_bf[:].rearrange("p q j -> p (q j)"), Q)
+        q_codes, q_scales = quantise("q", q_bf[:].rearrange("p q j -> p (q j)"), Q, tag="sq")
         scores = ps.tile([P, SLOTS], F32, name="scores")
         nc.tensor.matmul_mx(
             out=scores[:],
@@ -171,15 +179,14 @@ def tile_attend_blrscaled_soft_kernel(tc, query, keys_words, keys_scales, tab_wo
             stop=True,
         )
 
-        neg_max = tile("neg_max", [P, 1], F32)
-        nc.vector.tensor_reduce(out=neg_max[:], in_=scores[:], axis=AXIS.X, op=ALU.max, negate=True)
         factor = tile("factor", [P, CHUNKS * PAGES, PACK], F32)
-        nc.vector.tensor_tensor(
-            out=factor[:],
-            in0=inv_rms[:].rearrange("p (g t) -> p g t", t=PACK),
-            in1=gain_sb[:].rearrange("p (o t) -> p o t", o=1).to_broadcast([P, CHUNKS * PAGES, PACK]),
-            op=ALU.mult,
-        )
+        for first, pages, src in ((0, PAGES, inv_last[:]), (PAGES, (CHUNKS - 1) * PAGES, inv_rms[:, 0:early])):
+            nc.vector.tensor_tensor(
+                out=factor[:, first : first + pages],
+                in0=src.rearrange("p (g t) -> p g t", t=PACK),
+                in1=gain_sb[:].rearrange("p (o t) -> p o t", o=1).to_broadcast([P, pages, PACK]),
+                op=ALU.mult,
+            )
 
         hv = []
         for c in range(CHUNKS):
@@ -193,21 +200,24 @@ def tile_attend_blrscaled_soft_kernel(tc, query, keys_words, keys_scales, tab_wo
             hv.append(tile("hv%d" % c, [P, CHUNK, PACK], F32))
             nc.scalar.activation(out=hv[c][:].rearrange("p n t -> p (n t)"), in_=x[:].rearrange("p g j t -> p (g j t)"), func=ACT.Silu)
 
-        h_bf = [tile("h_bf%d" % c, [P, CHUNK, PACK], BF16) for c in range(CHUNKS)]
+        neg_max = tile("neg_max", [P, 1], F32)
+        nc.vector.tensor_reduce(out=neg_max[:], in_=scores[:], axis=AXIS.X, op=ALU.max, negate=True)
         c0 = ps.tile([P, SLOTS], F32, name="c0")
+        h_bf = [tile("h_bf%d" % h, [P, 2, CHUNK, PACK], BF16) for h in range(2)]
 
         def scale_rows(c):
-            nc.vector.tensor_tensor(
-                out=h_bf[c][:],
+            engine = nc.gpsimd if c == 0 else nc.vector
+            engine.tensor_tensor(
+                out=h_bf[c // 2][:, c % 2],
                 in0=hv[c][:],
                 in1=hsc_sb[:].rearrange("p (o t) -> p o t", o=1).to_broadcast([P, CHUNK, PACK]),
                 op=ALU.mult,
             )
 
-        def read_back(c):
-            h_codes, h_scales = quantise("h%d" % c, h_bf[c][:].rearrange("p n t -> p (n t)"), CHUNK)
+        def read_back(h):
+            h_codes, h_scales = quantise("h%d" % h, h_bf[h][:].rearrange("p c n t -> p (c n t)"), 2 * CHUNK)
             nc.tensor.matmul_mx(
-                out=c0[:, c * CHUNK : (c + 1) * CHUNK],
+                out=c0[:, h * 2 * CHUNK : (h + 1) * 2 * CHUNK],
                 lhsT=g_codes[:].bitcast(FP8X4),
                 lhsT_scale=g_scales[:],
                 rhs=h_codes[:].bitcast(FP8X4),
@@ -216,11 +226,11 @@ def tile_attend_blrscaled_soft_kernel(tc, query, keys_words, keys_scales, tab_wo
                 stop=True,
             )
 
-        scale_rows(0)
-        for c in range(1, CHUNKS):
+        for c in range(3):
             scale_rows(c)
-            read_back(c - 1)
-        read_back(CHUNKS - 1)
+        read_back(0)
+        scale_rows(3)
+        read_back(1)
 
         p = tile("p", [P, SLOTS], F32, tag="x%d" % (CHUNKS - 1))
         z = tile("z", [P, 1], F32)

@@ -25,7 +25,7 @@ PAGE = 16
 CHUNK = 128
 CHUNKS = SLOTS // CHUNK
 PAGES = CHUNK // PAGE
-OUT_COLS = (256, 512, 512, 512, 256)
+OUT_COLS = (256, 384, 448, 480, 480)
 
 FLOPS = 2 * 512 * SLOTS * (Q + R + Q)
 
@@ -119,7 +119,7 @@ def tile_attend_blrscaled_soft_kernel(tc, query, keys_words, keys_scales, tab_wo
             )
 
         zh = [ps.tile([P, PACK, CHUNK], F32, name="zh%d" % c) for c in range(CHUNKS)]
-        for c in (1, 2, 3, 0):
+        for c in (2, 3, 1, 0):
             cols = slice(c * CHUNK, (c + 1) * CHUNK)
             for t in range(PACK):
                 nc.tensor.matmul_mx(
@@ -135,19 +135,20 @@ def tile_attend_blrscaled_soft_kernel(tc, query, keys_words, keys_scales, tab_wo
         key_wg = gather("key_wg", key_w, U16)
 
         key_sg = gather("key_sg", key_s, U8)
-        early = (CHUNKS - 1) * PAGES * PACK
+        early = 2 * PAGES * PACK
         sq = tile("sq", [P, PAGE * early + P - early], F32)
         nc.gpsimd.memset(sq[:, PAGE * early :], 0.0)
         sq_view = sq[:, 0 : PAGE * early].rearrange("p (j c g t) -> p j c g t", j=PAGE, g=PAGES, t=PACK)
-        for c in range(1, CHUNKS):
+        for c in (2, 3):
             nc.scalar.activation(
-                out=sq_view[:, :, c - 1],
+                out=sq_view[:, :, c - 2],
                 in_=zh[c][:].rearrange("p t (g j) -> p j g t", j=PAGE),
                 func=ACT.Square,
                 scale=0.25,
             )
-        sq_last = tile("sq_last", [P, PAGES, PACK, PAGE], F32)
-        nc.scalar.activation(out=sq_last[:], in_=zh[0][:].rearrange("p t (g j) -> p g t j", j=PAGE), func=ACT.Square, scale=0.25)
+        sq_last = [tile("sq_last%d" % c, [P, PAGES, PACK, PAGE], F32) for c in range(2)]
+        for c in (1, 0):
+            nc.scalar.activation(out=sq_last[c][:], in_=zh[c][:].rearrange("p t (g j) -> p g t j", j=PAGE), func=ACT.Square, scale=0.25)
         mean_sq_t = ps.tile([P, P], F32, name="mean_sq_t")
         for j in range(PAGE):
             nc.tensor.matmul(
@@ -159,11 +160,17 @@ def tile_attend_blrscaled_soft_kernel(tc, query, keys_words, keys_scales, tab_wo
                 stop=(j == PAGE - 1),
             )
         g_codes, g_scales = quantise("g", g_bf[:].rearrange("p q j -> p (q j)"), Q)
-        mean_sq = tile("mean_sq", [P, PAGES * PACK], F32)
-        nc.vector.tensor_reduce(out=mean_sq[:], in_=sq_last[:].rearrange("p g t j -> p (g t) j"), axis=AXIS.X, op=ALU.add)
+        mean_sq = tile("mean_sq", [P, 2 * PAGES * PACK], F32)
+        for c in (1, 0):
+            nc.vector.tensor_reduce(
+                out=mean_sq[:, c * PAGES * PACK : (c + 1) * PAGES * PACK],
+                in_=sq_last[c][:].rearrange("p g t j -> p (g t) j"),
+                axis=AXIS.X,
+                op=ALU.add,
+            )
         inv_rms_t = tile("inv_rms_t", [P, P], F32)
         nc.scalar.activation(out=inv_rms_t[:], in_=mean_sq_t[:], func=ACT.Abs_reciprocal_sqrt, bias=0.1)
-        inv_last = tile("inv_last", [P, PAGES * PACK], F32)
+        inv_last = tile("inv_last", [P, 2 * PAGES * PACK], F32)
         nc.scalar.activation(out=inv_last[:], in_=mean_sq[:], func=ACT.Abs_reciprocal_sqrt, bias=0.1)
         inv_rms = ps.tile([P, P], F32, name="inv_rms")
         nc.tensor.transpose(inv_rms[:], inv_rms_t[:], ident[:])
@@ -180,7 +187,7 @@ def tile_attend_blrscaled_soft_kernel(tc, query, keys_words, keys_scales, tab_wo
         )
 
         factor = tile("factor", [P, CHUNKS * PAGES, PACK], F32)
-        for first, pages, src in ((0, PAGES, inv_last[:]), (PAGES, (CHUNKS - 1) * PAGES, inv_rms[:, 0:early])):
+        for first, pages, src in ((0, 2 * PAGES, inv_last[:]), (2 * PAGES, 2 * PAGES, inv_rms[:, 0:early])):
             nc.vector.tensor_tensor(
                 out=factor[:, first : first + pages],
                 in0=src.rearrange("p (g t) -> p g t", t=PACK),

from contextlib import ExitStack

import concourse.mybir as mybir
from concourse.masks import make_identity

F32 = mybir.dt.float32
BF16 = mybir.dt.bfloat16
I32 = mybir.dt.int32
U32 = mybir.dt.uint32
U16 = mybir.dt.uint16
U8 = mybir.dt.uint8
FP8X4 = mybir.dt.float8_e4m3fn_x4
FP4X4 = mybir.dt.float4_e2m1fn_x4
ALU = mybir.AluOpType
ACT = mybir.ActivationFunctionType
AXIS = mybir.AxisListType

P = 128
PACK = 4
T = 2048
SLOTS = 512
R = 512
Q = 128
PAGE = 16
CHUNK = 128
CHUNKS = SLOTS // CHUNK
PAGES = CHUNK // PAGE
OUT_COLS = (256, 384, 448, 480, 480)

FLOPS = 2 * 512 * SLOTS * (Q + R + Q)


def tile_attend_blrscaled_soft_kernel(tc, query, keys_words, keys_scales, tab_words, tab_scales, w1, gain, gout, hsc, old, offs, out):
    nc = tc.nc
    with ExitStack() as ctx:
        sb = ctx.enter_context(tc.tile_pool(name="sb", bufs=1))
        ps = ctx.enter_context(tc.psum_pool(name="ps", bufs=1))

        def tile(name, shape, dtype, tag=None):
            return sb.tile(shape, dtype, name=name, tag=tag or name, align_bytes=64)

        offsets = sb.tile([P, SLOTS // 16], U16, name="offsets")
        tab_w = tile("tab_w", [P, T], U16)
        tab_s = tile("tab_s", [P, T], U8)
        key_w = tile("key_w", [P, T], U16)
        key_s = tile("key_s", [P, T], U8)
        window = tile("window", [P, T], F32)

        nc.vector.memset(tab_s[:].bitcast(I32), 0)
        nc.vector.memset(key_s[:].bitcast(I32), 0)
        nc.vector.memset(window[:], 0.0)

        def load_scales(dst, src):
            rows = src[0].bitcast(I32)
            for quad in range(4):
                nc.sync.dma_start(out=dst[:].bitcast(I32)[32 * quad : 32 * quad + 4, :], in_=rows[4 * quad : 4 * quad + 4, :])

        nc.sync.dma_start(offsets[:], offs)
        nc.sync.dma_start(out=tab_w[:].bitcast(I32), in_=tab_words[0].bitcast(I32))
        load_scales(tab_s, tab_scales)
        half = R // 2
        w_raw = [tile("w_raw%d" % h, [P, PACK, half], F32) for h in range(2)]
        w_rows = w1.rearrange("(p j) r -> p j r", j=PACK)
        for h in range(2):
            nc.sync.dma_start(out=w_raw[h][:], in_=w_rows[:, :, h * half : (h + 1) * half])
        q_raw = tile("q_raw", [P, PACK, Q], F32)
        g_raw = tile("g_raw", [P, PACK, Q], F32)
        nc.sync.dma_start(out=q_raw[:], in_=query.rearrange("(p j) q -> p j q", j=PACK))
        nc.sync.dma_start(out=g_raw[:], in_=gout.rearrange("(p j) q -> p j q", j=PACK))
        nc.sync.dma_start(out=key_w[:].bitcast(I32), in_=keys_words[0].bitcast(I32))
        load_scales(key_s, keys_scales)
        gain_sb = tile("gain_sb", [P, PACK], F32)
        hsc_sb = tile("hsc_sb", [P, PACK], F32)
        nc.sync.dma_start(out=gain_sb[:], in_=gain.rearrange("(p j) o -> p (j o)", j=PACK))
        nc.sync.dma_start(out=hsc_sb[:], in_=hsc.rearrange("(p j) o -> p (j o)", j=PACK))
        old_sb = tile("old_sb", [P, T], F32)
        nc.sync.dma_start(out=old_sb[:], in_=old)

        consts = tile("consts", [P, 2], F32)
        nc.gpsimd.memset(consts[:, 0:1], 512.0)
        nc.gpsimd.memset(consts[:, 1:2], -1.0)
        warm = tile("warm", [P, 1], F32)
        nc.scalar.activation(out=warm[:], in_=consts[:, 0:1], func=ACT.Abs_reciprocal_sqrt)
        ident = tile("ident", [P, P], F32)
        make_identity(nc, ident[:])

        def gather(name, src, dtype):
            dst = tile(name, [P, SLOTS], dtype)
            nc.vector.tensor_copy(dst[:], src[:].indirect(offsets[:]))
            return dst

        def quantise(name, src, words, tag=None):
            codes = tile(name + "_codes", [P, words], U32, tag=tag)
            scales = tile(name + "_scales", [P, words], U8)
            nc.vector.quantize_mx(out=codes[:].bitcast(FP8X4), scales=scales[:], in_=src)
            return codes, scales

        tab_wg = gather("tab_wg", tab_w, U16)
        tab_sg = gather("tab_sg", tab_s, U8)

        w_bf = tile("w_bf", [P, PACK, P, PACK], BF16)
        mh = P // 2
        nc.scalar.copy(
            out=w_bf[:, :, 0:mh, :].rearrange("p t m j -> p m j t"),
            in_=w_raw[0][:].rearrange("p j (m t) -> p m j t", t=PACK),
        )
        share = 20
        late = w_raw[1][:].rearrange("p j (m t) -> p m j t", t=PACK)
        nc.scalar.copy(out=w_bf[:, :, mh : mh + share, :].rearrange("p t m j -> p m j t"), in_=late[:, 0:share])
        nc.vector.tensor_copy(out=w_bf[:, :, mh + share : P, :].rearrange("p t m j -> p m j t"), in_=late[:, share:mh])
        w_mx = [quantise("w%d" % t, w_bf[:, t].rearrange("p m j -> p (m j)"), P) for t in range(PACK)]

        q_bf = tile("q_bf", [P, Q, PACK], BF16)
        g_bf = tile("g_bf", [P, Q, PACK], BF16)
        for dst, src in ((q_bf, q_raw), (g_bf, g_raw)):
            nc.scalar.copy(
                out=dst[:].rearrange("p (c i) j -> p c j i", i=4),
                in_=src[:].rearrange("p j (c i) -> p c j i", i=4),
            )

        zh = [ps.tile([P, PACK, CHUNK], F32, name="zh%d" % c) for c in range(CHUNKS)]
        for c in (2, 3, 1, 0):
            cols = slice(c * CHUNK, (c + 1) * CHUNK)
            for t in range(PACK):
                nc.tensor.matmul_mx(
                    out=zh[c][:, t, :],
                    lhsT=w_mx[t][0][:].bitcast(FP8X4),
                    lhsT_scale=w_mx[t][1][:],
                    rhs=tab_wg[:, cols].bitcast(FP4X4),
                    rhs_scale=tab_sg[:, cols],
                    start=True,
                    stop=True,
                )

        key_wg = gather("key_wg", key_w, U16)

        key_sg = gather("key_sg", key_s, U8)
        early = 2 * PAGES * PACK
        sq = tile("sq", [P, PAGE * early + P - early], F32)
        nc.gpsimd.memset(sq[:, PAGE * early :], 0.0)
        sq_view = sq[:, 0 : PAGE * early].rearrange("p (j c g t) -> p j c g t", j=PAGE, g=PAGES, t=PACK)
        for c in (2, 3):
            nc.scalar.activation(
                out=sq_view[:, :, c - 2],
                in_=zh[c][:].rearrange("p t (g j) -> p j g t", j=PAGE),
                func=ACT.Square,
                scale=0.25,
            )
        sq_last = [tile("sq_last%d" % c, [P, PAGES, PACK, PAGE], F32) for c in range(2)]
        for c in (1, 0):
            nc.scalar.activation(out=sq_last[c][:], in_=zh[c][:].rearrange("p t (g j) -> p g t j", j=PAGE), func=ACT.Square, scale=0.25)
        mean_sq_t = ps.tile([P, P], F32, name="mean_sq_t")
        for j in range(PAGE):
            nc.tensor.matmul(
                out=mean_sq_t[:],
                lhsT=sq[:, j * early : j * early + P],
                rhs=ident[:],
                is_transpose=True,
                start=(j == 0),
                stop=(j == PAGE - 1),
            )
        g_codes, g_scales = quantise("g", g_bf[:].rearrange("p q j -> p (q j)"), Q)
        mean_sq = tile("mean_sq", [P, 2 * PAGES * PACK], F32)
        for c in (1, 0):
            nc.vector.tensor_reduce(
                out=mean_sq[:, c * PAGES * PACK : (c + 1) * PAGES * PACK],
                in_=sq_last[c][:].rearrange("p g t j -> p (g t) j"),
                axis=AXIS.X,
                op=ALU.add,
            )
        inv_rms_t = tile("inv_rms_t", [P, P], F32)
        nc.scalar.activation(out=inv_rms_t[:], in_=mean_sq_t[:], func=ACT.Abs_reciprocal_sqrt, bias=0.1)
        inv_last = tile("inv_last", [P, 2 * PAGES * PACK], F32)
        nc.scalar.activation(out=inv_last[:], in_=mean_sq[:], func=ACT.Abs_reciprocal_sqrt, bias=0.1)
        inv_rms = ps.tile([P, P], F32, name="inv_rms")
        nc.tensor.transpose(inv_rms[:], inv_rms_t[:], ident[:])
        q_codes, q_scales = quantise("q", q_bf[:].rearrange("p q j -> p (q j)"), Q, tag="sq")
        scores = ps.tile([P, SLOTS], F32, name="scores")
        nc.tensor.matmul_mx(
            out=scores[:],
            lhsT=q_codes[:].bitcast(FP8X4),
            lhsT_scale=q_scales[:],
            rhs=key_wg[:].bitcast(FP4X4),
            rhs_scale=key_sg[:],
            start=True,
            stop=True,
        )

        factor = tile("factor", [P, CHUNKS * PAGES, PACK], F32)
        for first, pages, src in ((0, 2 * PAGES, inv_last[:]), (2 * PAGES, 2 * PAGES, inv_rms[:, 0:early])):
            nc.vector.tensor_tensor(
                out=factor[:, first : first + pages],
                in0=src.rearrange("p (g t) -> p g t", t=PACK),
                in1=gain_sb[:].rearrange("p (o t) -> p o t", o=1).to_broadcast([P, pages, PACK]),
                op=ALU.mult,
            )

        hv = []
        for c in range(CHUNKS):
            x = tile("x%d" % c, [P, PAGES, PAGE, PACK], F32)
            nc.vector.tensor_tensor(
                out=x[:],
                in0=zh[c][:].rearrange("p t (g j) -> p g j t", j=PAGE),
                in1=factor[:, c * PAGES : (c + 1) * PAGES, :].rearrange("p g (o t) -> p g o t", o=1).to_broadcast([P, PAGES, PAGE, PACK]),
                op=ALU.mult,
            )
            hv.append(tile("hv%d" % c, [P, CHUNK, PACK], F32))
            nc.scalar.activation(out=hv[c][:].rearrange("p n t -> p (n t)"), in_=x[:].rearrange("p g j t -> p (g j t)"), func=ACT.Silu)

        neg_max = tile("neg_max", [P, 1], F32)
        nc.vector.tensor_reduce(out=neg_max[:], in_=scores[:], axis=AXIS.X, op=ALU.max, negate=True)
        c0 = ps.tile([P, SLOTS], F32, name="c0")
        h_bf = [tile("h_bf%d" % h, [P, 2, CHUNK, PACK], BF16) for h in range(2)]

        def scale_rows(c):
            engine = nc.gpsimd if c == 0 else nc.vector
            engine.tensor_tensor(
                out=h_bf[c // 2][:, c % 2],
                in0=hv[c][:],
                in1=hsc_sb[:].rearrange("p (o t) -> p o t", o=1).to_broadcast([P, CHUNK, PACK]),
                op=ALU.mult,
            )

        def read_back(h):
            h_codes, h_scales = quantise("h%d" % h, h_bf[h][:].rearrange("p c n t -> p (c n t)"), 2 * CHUNK)
            nc.tensor.matmul_mx(
                out=c0[:, h * 2 * CHUNK : (h + 1) * 2 * CHUNK],
                lhsT=g_codes[:].bitcast(FP8X4),
                lhsT_scale=g_scales[:],
                rhs=h_codes[:].bitcast(FP8X4),
                rhs_scale=h_scales[:],
                start=True,
                stop=True,
            )

        for c in range(3):
            scale_rows(c)
        read_back(0)
        scale_rows(3)
        read_back(1)

        p = tile("p", [P, SLOTS], F32, tag="x%d" % (CHUNKS - 1))
        z = tile("z", [P, 1], F32)
        nc.scalar.activation(out=p[:], in_=scores[:], func=ACT.Exp, bias=neg_max[:], accum_out=z[:])
        inv_z = tile("inv_z", [P, 1], F32)
        nc.vector.reciprocal(out=inv_z[:], in_=z[:])
        coef = tile("coef", [P, 2], F32)
        nc.vector.tensor_scalar(out=coef[:], in0=consts[:], scalar1=inv_z[:], scalar2=None, op0=ALU.mult)

        cp = tile("cp", [P, SLOTS], F32)
        total = tile("total", [P, 1], F32)
        nc.vector.scalar_tensor_tensor(out=cp[:], in0=c0[:], scalar=coef[:, 0:1], in1=p[:], op0=ALU.mult, op1=ALU.mult, accum_out=total[:])
        shift = tile("shift", [P, SLOTS], F32)
        nc.vector.tensor_scalar(out=shift[:], in0=p[:], scalar1=total[:], scalar2=coef[:, 1:2], op0=ALU.mult, op1=ALU.mult)
        nc.vector.tensor_tensor(out=window[:].indirect(offsets[:]), in0=cp[:], in1=shift[:], op=ALU.add)

        for n, width in enumerate(OUT_COLS):
            first = sum(OUT_COLS[:n])
            cols = slice(first, first + width)
            res = tile("res%d" % n, [P, width], F32)
            nc.vector.tensor_tensor(out=res[:], in0=window[:, cols], in1=old_sb[:, cols], op=ALU.add)
            queue = nc.sync if n % 2 == 0 else nc.scalar
            queue.dma_start(out=out[:, cols], in_=res[:])
